import numpy as np
import ml_dtypes


def mxq(x, axis, fmt="e4m3"):
    dtype, down = {"e4m3": (ml_dtypes.float8_e4m3fn, 7), "e5m2": (ml_dtypes.float8_e5m2, 14)}[fmt]
    v = np.moveaxis(np.asarray(x, np.float32).astype(ml_dtypes.bfloat16).astype(np.float64), axis, -1)
    blocks = v.reshape(v.shape[:-1] + (-1, 32))
    amax = np.abs(blocks).max(-1, keepdims=True)
    byte = np.maximum(np.where(amax > 0, np.frexp(amax)[1] - 1 + 127, 0) - down, 1)
    scale = np.exp2(byte - 127.0)
    codes = (blocks / scale).astype(np.float32).astype(dtype).astype(np.float64)
    return np.moveaxis((codes * scale).reshape(v.shape), -1, axis)


WIDE = False


def mx_kscale(k):
    if not WIDE:
        return np.ones(k)
    levels = np.array([10, -10, 5, -5, 0])
    if k % 512:
        return np.exp2(np.random.permutation(np.resize(levels, k // 32))).repeat(32)
    a = np.empty((k // 512, 16))
    for p in range(k // 512):
        a[p, :8] = np.random.permutation(np.resize(levels, 8))
        for g in range(8):
            far = levels[np.abs(levels - a[p, g]) >= 10]
            a[p, g + 8] = far[np.random.randint(len(far))]
    return np.exp2(a.ravel()).repeat(32)


BF16 = ml_dtypes.bfloat16


def bf(x):
    return np.asarray(x, np.float32).astype(BF16)


def f64(x):
    return np.asarray(x).astype(np.float64)


E2M1 = np.array([0.0, 0.5, 1.0, 1.5, 2.0, 3.0, 4.0, 6.0, -0.0, -0.5, -1.0, -1.5, -2.0, -3.0, -4.0, -6.0])


def pack_weight(w, fmt):
    k, n = w.shape
    w = f64(bf(w)).reshape(k // 32, 32, n)
    amax = np.abs(w).max(1)
    if fmt == "e4m3":
        byte = np.frexp(amax)[1] - 1 + 127 - 7
    else:
        mant, ex = np.frexp(amax / 6.0)
        byte = np.where(mant > 0.5, ex, ex - 1) + 127
    byte = np.clip(np.where(amax > 0, byte, 1), 1, 254)
    scaled = (w * np.exp2(127.0 - byte)[:, None, :]).reshape(k, n).astype(np.float32)
    by_word = np.ascontiguousarray(scaled.reshape(k // 512, 128, 4, n).transpose(0, 1, 3, 2))
    if fmt == "e4m3":
        words = by_word.astype(ml_dtypes.float8_e4m3fn).view(np.uint8)
    else:
        c = by_word.astype(ml_dtypes.float4_e2m1fn).view(np.uint8) & 0xF
        words = c[..., 0::2] | (c[..., 1::2] << 4)
    return np.ascontiguousarray(words), np.ascontiguousarray(byte.astype(np.uint8).reshape(k // 512, 16, n))


def unpack_weight(words, scales, fmt):
    g, p, n, _ = words.shape
    if fmt == "e4m3":
        vals = np.ascontiguousarray(words).view(ml_dtypes.float8_e4m3fn).astype(np.float64)
    else:
        nib = np.empty((g, p, n, 4), np.uint8)
        nib[..., 0::2] = words & 0xF
        nib[..., 1::2] = words >> 4
        vals = E2M1[nib]
    vals = vals * np.repeat(np.exp2(scales.astype(np.float64) - 127.0), 8, axis=1)[..., None]
    return vals.transpose(0, 1, 3, 2).reshape(g * 512, n)


N, D, F, T = 1024, 1024, 1024, 512

NEG_SLOPE = 0.25
LR_DIV = 32.0


def leaky_slope(a):
    return np.where(a > 0, 1.0, NEG_SLOPE)


def synthetic_gradient(h, m, t, c):
    return (mxq(h, 1, "e4m3") @ m) + (mxq(t, 1, "e4m3") @ c)


def draw0():
    s, u, v = mx_kscale(F), mx_kscale(T), mx_kscale(N)
    x = bf(np.random.standard_normal((N, D)) * (LR_DIV / np.sqrt(N)) / v[:, None])
    a = bf(np.random.standard_normal((N, F)) * s)
    m_words, m_scales = pack_weight(np.random.standard_normal((F, F)) / np.sqrt(F) / s[:, None], "e4m3")
    t = bf(np.random.standard_normal((N, T)) * u)
    c_words, c_scales = pack_weight(np.random.standard_normal((T, F)) / np.sqrt(T) / u[:, None], "e4m3")
    return {
        "x": x,
        "a": a,
        "m_words": m_words,
        "m_scales": m_scales,
        "t": t,
        "c_words": c_words,
        "c_scales": c_scales,
        "r": bf((1.0 + 0.1 * np.random.standard_normal(N)) * v),
        "w": bf(0.5 * np.random.standard_normal((D, F))),
    }


def core(x, a, m_words, m_scales, t, c_words, c_scales, r, w):
    a = f64(a)
    k = leaky_slope(a)
    h = a * k
    m = unpack_weight(m_words, m_scales, "e4m3")
    c = unpack_weight(c_words, c_scales, "e4m3")
    sg = synthetic_gradient(h, m, f64(t), c)
    d = sg * k * f64(r)[:, None]
    upd = mxq(f64(x), 0, "e4m3").T @ mxq(d, 0, "e4m3")
    return f64(w) - upd / LR_DIV


def e4m3fn_bytes(y):
    return np.clip(np.asarray(y, np.float64), -448.0, 448.0).astype(np.float32).astype(ml_dtypes.float8_e4m3fn).view(np.uint8)


def e4m3fn_values(b):
    return np.asarray(b, np.uint8).view(ml_dtypes.float8_e4m3fn).astype(np.float64)


def setup_inputs():
    d = draw0()
    x0 = np.asarray(d['x']).astype(np.float64)
    s = (np.max(np.abs(x0), axis=(1,), keepdims=True) / 448.0).astype(np.float32)
    out = {}
    for k, v in d.items():
        if k == 'x':
            out['x_bytes'] = e4m3fn_bytes(x0 / s.astype(np.float64))
            out['x_scale'] = s
        else:
            out[k] = v
    return out


def reference(x_bytes, x_scale, a, m_words, m_scales, t, c_words, c_scales, r, w):
    return core(e4m3fn_values(x_bytes) * x_scale.astype(np.float64), a, m_words, m_scales, t, c_words, c_scales, r, w)

@@ -1,0 +1,408 @@
+from contextlib import ExitStack
+
+import concourse.mybir as mybir
+from concourse.masks import make_identity
+
+N, D, F, T = 1024, 1024, 1024, 512
+FLOPS = 2 * N * F * (F + T) + 2 * N * D * F
+
+F32 = mybir.dt.float32
+BF16 = mybir.dt.bfloat16
+I32 = mybir.dt.int32
+U32 = mybir.dt.uint32
+U8 = mybir.dt.uint8
+FP8 = mybir.dt.float8_e4m3fn
+FP8X4 = mybir.dt.float8_e4m3fn_x4
+ALU = mybir.AluOpType
+COPY = mybir.ActivationFunctionType.Copy
+
+P = 128
+PACK = 4
+HALF = 512
+QUARTER = 256
+BANKS = 8
+NEG_SLOPE = 0.25
+STEP = -1.0 / 32.0
+
+
+def tile_conditionalsyntheticgradientweightupdate_w8_kernel(
+    tc, x_bytes, x_scale, a, m_words, m_scales, t, c_words, c_scales, r, w, out
+):
+    nc = tc.nc
+    with ExitStack() as ctx:
+        keep = ctx.enter_context(tc.tile_pool(name="keep", bufs=1))
+        ring = ctx.enter_context(tc.tile_pool(name="ring", bufs=3))
+        psum = ctx.enter_context(tc.psum_pool(name="psum", bufs=1))
+        ctx.enter_context(tc.manual_schedule(engines={mybir.EngineType.SP}))
+
+        taken = []
+
+        def next_bank():
+            bank = psum.tile([P, HALF], F32, name="bank%d" % len(taken), tag="bank%d" % (len(taken) % BANKS))
+            taken.append(bank)
+            return bank
+
+        a_rows = a.rearrange("(g p j) f -> g p (j f)", p=P, j=PACK)
+        t_rows = t.rearrange("(g p j) f -> g p (j f)", p=P, j=PACK)
+        x_rows = x_bytes.rearrange("(g p j) f -> g p j f", p=P, j=PACK)
+        a_sb, t_sb, x_sb, w_sb, wt_codes = {}, {}, {}, {}, {}
+
+        def load_a(s, count):
+            tile = keep.tile([P, count * F], BF16, name="a%d" % s, align_bytes=64)
+            g, j = divmod(s, PACK)
+            nc.sync.dma_start(out=tile[:], in_=a_rows[g][:, j * F : (j + count) * F])
+            for i in range(count):
+                a_sb[s + i] = tile[:, i * F : (i + 1) * F]
+
+        def load_t(pair):
+            tile = keep.tile([P, 2 * T], BF16, name="t%d" % pair, align_bytes=64)
+            g, jj = divmod(pair, 2)
+            nc.sync.dma_start(out=tile[:], in_=t_rows[g][:, jj * 2 * T : (jj + 1) * 2 * T])
+            t_sb[pair] = tile
+
+        def load_x(g, side):
+            tile = keep.tile([P, PACK, HALF], U8, name="xbytes%d_%d" % (g, side), align_bytes=64)
+            nc.sync.dma_start(out=tile[:], in_=x_rows[g][:, :, side * HALF : (side + 1) * HALF])
+            x_sb[g, side] = tile
+
+        def load_w(pair):
+            tile = keep.tile([P, 2, F], BF16, name="w%d" % pair, align_bytes=64)
+            rows = w[pair * 2 * P : (pair + 1) * 2 * P, :].rearrange("(i p) f -> p i f", p=P)
+            nc.sync.dma_start(out=tile[:], in_=rows)
+            w_sb[2 * pair] = tile[:, 0, :]
+            w_sb[2 * pair + 1] = tile[:, 1, :]
+
+        word_sources = [m_words[0], m_words[1], c_words[0]]
+
+        def load_words(q, half):
+            tile = keep.tile([P, HALF], U32, name="words%d_%d" % (q, half), align_bytes=64)
+            src = word_sources[q].rearrange("p n t -> p (n t)")[:, half * HALF * PACK : (half + 1) * HALF * PACK]
+            nc.sync.dma_start(out=tile[:].bitcast(I32), in_=src.bitcast(I32))
+            wt_codes[q, half] = tile
+
+        wt_scales = keep.tile([P, F], U8, name="wt_scales", align_bytes=64)
+        ident = keep.tile([P, P], F32, name="ident")
+        r_raw = keep.tile([P, 2, PACK], BF16, name="r_raw")
+        r_sb = keep.tile([P, 2 * PACK], F32, name="r_sb")
+        xs_sb = keep.tile([P, 2, PACK], F32, name="xs_sb")
+
+        def load_m_scales(quad):
+            nc.sync.dma_start(
+                out=wt_scales[32 * quad : 32 * quad + 8, :].bitcast(I32),
+                in_=m_scales[:, 4 * quad : 4 * quad + 4, :].bitcast(I32),
+            )
+
+        def load_c_scales(quad):
+            nc.gpsimd.dma_start(
+                out=wt_scales[32 * quad + 8 : 32 * quad + 12, :].bitcast(I32),
+                in_=c_scales[0, 4 * quad : 4 * quad + 4, :].bitcast(I32),
+            )
+
+        nc.vector.memset(wt_scales[:].bitcast(I32), 0)
+        make_identity(nc, ident[:])
+        for quad in range(4):
+            load_c_scales(quad)
+
+        load_a(0, 1)
+        nc.scalar.dma_start(out=r_raw[:], in_=r.rearrange("(g p j) -> p g j", p=P, j=PACK))
+        nc.scalar.dma_start(out=xs_sb[:], in_=x_scale.rearrange("(g p j) o -> p g (j o)", p=P, j=PACK))
+        load_x(0, 0)
+        load_a(1, 1)
+        load_t(0)
+        load_a(2, 2)
+        load_t(1)
+        for quad in range(4):
+            load_m_scales(quad)
+        load_x(0, 1)
+        for q in (2, 0, 1):
+            load_words(q, 0)
+        load_a(4, 2)
+        load_t(2)
+        for q in (2, 0, 1):
+            load_words(q, 1)
+        load_a(6, 2)
+        load_t(3)
+        load_x(1, 0)
+        load_x(1, 1)
+        for pair in range(4):
+            load_w(pair)
+
+        nc.scalar.activation(out=r_sb[:], in_=r_raw[:].rearrange("p g j -> p (g j)"), func=COPY)
+
+        k_sb, h_sb, banks, turned, act_codes, act_scales = {}, {}, {}, {}, {}, {}
+
+        def slope(s, lo=0, hi=F):
+            if s not in k_sb:
+                k_sb[s] = keep.tile([P, F], BF16, name="k%d" % s, align_bytes=64)
+            nc.vector.tensor_scalar(
+                out=k_sb[s][:, lo:hi], in0=a_sb[s][:, lo:hi], scalar1=0.0, scalar2=NEG_SLOPE, op0=ALU.is_gt, op1=ALU.max
+            )
+
+        def leaky(s, lo=0, hi=F):
+            if s not in h_sb:
+                h_sb[s] = ring.tile([P, F], BF16, name="h%d" % s, tag="h", align_bytes=64)
+            nc.vector.tensor_tensor(out=h_sb[s][:, lo:hi], in0=a_sb[s][:, lo:hi], in1=k_sb[s][:, lo:hi], op=ALU.mult)
+
+        def turn(unit):
+            kind, index = unit
+            words = (h_sb if kind == "h" else t_sb)[index][:].bitcast(F32)
+            bank = next_bank()
+            for part in range(2):
+                for u in range(2):
+                    col = (2 * part + u) * P
+                    nc.tensor.transpose(
+                        bank[:, col : col + P], words[:, 2 * P * part + u : 2 * P * (part + 1) : 2], ident[:]
+                    )
+            banks[unit] = bank
+
+        def drain(unit):
+            tile = ring.tile([P, 2 * HALF], BF16, name="turned_%s%d" % unit, tag="turned", bufs=4, align_bytes=64)
+            nc.scalar.copy(
+                out=tile[:].bitcast(F32).rearrange("p (a n u) -> p a n u", a=2, u=2),
+                in_=banks[unit][:].rearrange("p (a u n) -> p a n u", a=2, u=2),
+            )
+            turned[unit] = tile
+
+        def quantize(name, source):
+            width = source.shape[1] // PACK
+            codes = keep.tile([P, width], U32, name=name + "_codes", align_bytes=64)
+            scales = keep.tile([P, width], U8, name=name + "_scales", align_bytes=64)
+            nc.vector.quantize_mx(out=codes[:].bitcast(FP8X4), scales=scales[:], in_=source)
+            return codes, scales
+
+        def quant_act(unit):
+            act_codes[unit], act_scales[unit] = quantize("act_%s%d" % unit, turned[unit][:])
+
+        sg_bank, d_planes, d_mixed, d_q = {}, {}, {}, {}
+
+        def predict(s, half):
+            bank = next_bank()
+            passes = [(("t", s // 2), s % 2, 2), (("h", s), 0, 0), (("h", s), 1, 1)]
+            for n, (unit, part, q) in enumerate(passes):
+                cols = slice(part * P, (part + 1) * P)
+                nc.tensor.matmul_mx(
+                    out=bank[:],
+                    lhsT=act_codes[unit][:, cols].bitcast(FP8X4),
+                    lhsT_scale=act_scales[unit][:, cols],
+                    rhs=wt_codes[q, half][:].bitcast(FP8X4),
+                    rhs_scale=wt_scales[4 * q :, half * HALF : (half + 1) * HALF],
+                    start=(n == 0),
+                    stop=(n == len(passes) - 1),
+                )
+            sg_bank[s, half] = bank
+
+        def grad(s, half):
+            g, j = divmod(s, PACK)
+            if j == 0:
+                d_planes[g, half] = ring.tile(
+                    [P, PACK, HALF], BF16, name="dpl%d_%d" % (g, half), tag="dpl", bufs=3, align_bytes=64
+                )
+            nc.vector.scalar_tensor_tensor(
+                out=d_planes[g, half][:, j, :],
+                in0=sg_bank[s, half][:],
+                scalar=r_sb[:, s : s + 1],
+                in1=k_sb[s][:, half * HALF : (half + 1) * HALF],
+                op0=ALU.mult,
+                op1=ALU.mult,
+            )
+
+        def interleave(engine, mixed, planes, lo, hi):
+            dst = mixed[:].rearrange("p (n j) -> p n j", j=PACK)[:, lo:hi, :]
+            src = planes[:, :, lo:hi].rearrange("p j n -> p n j")
+            if engine == "vector":
+                nc.vector.tensor_copy(out=dst, in_=src)
+            else:
+                nc.scalar.copy(out=dst, in_=src)
+
+        def mix_d(engine, g, half, lo, hi):
+            if (g, half) not in d_mixed:
+                d_mixed[g, half] = ring.tile(
+                    [P, PACK * HALF], BF16, name="dmix%d_%d" % (g, half), tag="dmix", bufs=2, align_bytes=64
+                )
+            interleave(engine, d_mixed[g, half], d_planes[g, half], lo, hi)
+
+        def quant_d(g, half):
+            d_q[g, half] = quantize("d%d_%d" % (g, half), d_mixed[g, half][:])
+
+        x_planes, x_mixed, x_q = {}, {}, {}
+
+        def widen(engine, g, piece, j):
+            if j == 0:
+                x_planes[g, piece] = ring.tile(
+                    [P, PACK, QUARTER], BF16, name="xpl%d_%d" % (g, piece), tag="xpl", bufs=4, align_bytes=64
+                )
+            side, part = divmod(piece, 2)
+            src = x_sb[g, side][:, j, part * QUARTER : (part + 1) * QUARTER].bitcast(FP8)
+            dst = x_planes[g, piece][:, j, :]
+            if engine == "vector":
+                nc.vector.tensor_scalar(out=dst, in0=src, scalar1=xs_sb[:, g, j : j + 1], scalar2=None, op0=ALU.mult)
+            else:
+                nc.scalar.activation(out=dst, in_=src, func=COPY, scale=xs_sb[:, g, j : j + 1])
+
+        def widen4(engine, g, piece):
+            for j in range(PACK):
+                widen(engine, g, piece, j)
+
+        def mix_x(engine, g, piece):
+            x_mixed[g, piece] = ring.tile(
+                [P, PACK * QUARTER], BF16, name="xmix%d_%d" % (g, piece), tag="xmix", bufs=4, align_bytes=64
+            )
+            interleave(engine, x_mixed[g, piece], x_planes[g, piece], 0, QUARTER)
+
+        def quant_x(g, piece):
+            x_q[g, piece] = quantize("x%d_%d" % (g, piece), x_mixed[g, piece][:])
+
+        upd_bank = {}
+
+        def update(i, half, g):
+            if g == 0:
+                upd_bank[i, half] = next_bank()
+            piece, part = divmod(i, 2)
+            cols = slice(part * P, (part + 1) * P)
+            nc.tensor.matmul_mx(
+                out=upd_bank[i, half][:],
+                lhsT=x_q[g, piece][0][:, cols].bitcast(FP8X4),
+                lhsT_scale=x_q[g, piece][1][:, cols],
+                rhs=d_q[g, half][0][:].bitcast(FP8X4),
+                rhs_scale=d_q[g, half][1][:],
+                start=(g == 0),
+                stop=(g == 1),
+            )
+
+        def finish(i, half):
+            cols = slice(half * HALF, (half + 1) * HALF)
+            result = ring.tile([P, HALF], F32, name="res%d_%d" % (i, half), tag="res", bufs=8)
+            nc.vector.scalar_tensor_tensor(
+                out=result[:], in0=upd_bank[i, half][:], scalar=STEP, in1=w_sb[i][:, cols], op0=ALU.mult, op1=ALU.add
+            )
+            nc.sync.dma_start(out=out[i * P : (i + 1) * P, cols], in_=result[:])
+
+        S, V = "scalar", "vector"
+
+        def prepare(s):
+            slope(s)
+            slope(s + 1)
+            leaky(s)
+            leaky(s + 1)
+
+        def units(s):
+            return (("h", s), ("t", s // 2), ("h", s + 1))
+
+        def each(step, items):
+            for item in items:
+                step(item)
+
+        def both(i):
+            for g in range(2):
+                for half in range(2):
+                    update(i, half, g)
+
+        for s in range(2):
+            slope(s, 0, HALF)
+            slope(s, HALF, F)
+            leaky(s, 0, HALF)
+            leaky(s, HALF, F)
+            turn(("h", s))
+        turn(("t", 0))
+        widen4(S, 0, 1)
+        widen4(V, 0, 0)
+        drain(("h", 0))
+        mix_x(S, 0, 1)
+        drain(("h", 1))
+        drain(("t", 0))
+        prepare(2)
+        each(turn, units(2))
+        mix_x(V, 0, 0)
+        quant_act(("h", 0))
+        quant_act(("h", 1))
+        quant_act(("t", 0))
+        predict(0, 0)
+        predict(1, 0)
+        widen4(S, 0, 2)
+        each(drain, units(2))
+        quant_x(0, 0)
+        quant_x(0, 1)
+        each(quant_act, units(2))
+        predict(2, 0)
+        predict(3, 0)
+        mix_x(S, 0, 2)
+        widen4(S, 0, 3)
+        prepare(4)
+        each(turn, units(4))
+        mix_x(S, 0, 3)
+        for s in range(4):
+            grad(s, 0)
+        each(drain, units(4))
+        predict(0, 1)
+        predict(1, 1)
+        prepare(6)
+        each(turn, units(6))
+        mix_d(S, 0, 0, 0, QUARTER)
+        each(quant_act, units(4))
+        each(drain, units(6))
+        grad(0, 1)
+        grad(1, 1)
+        predict(4, 0)
+        predict(5, 0)
+        mix_d(S, 0, 0, QUARTER, HALF)
+        widen4(S, 1, 0)
+        each(quant_act, units(6))
+        predict(6, 0)
+        predict(7, 0)
+        quant_x(0, 2)
+        quant_x(0, 3)
+        mix_x(S, 1, 0)
+        quant_d(0, 0)
+        for s in range(4, 8):
+            grad(s, 0)
+        predict(2, 1)
+        predict(3, 1)
+        for s in range(4, 8):
+            predict(s, 1)
+        widen4(S, 1, 1)
+        mix_d(S, 1, 0, 0, HALF)
+        quant_x(1, 0)
+        grad(2, 1)
+        grad(3, 1)
+        mix_d(S, 0, 1, 0, HALF)
+        mix_x(V, 1, 1)
+        grad(4, 1)
+        quant_d(1, 0)
+        grad(5, 1)
+        quant_x(1, 1)
+        for i in range(4):
+            update(i, 0, 0)
+            update(i, 0, 1)
+        grad(6, 1)
+        grad(7, 1)
+        quant_d(0, 1)
+        mix_d(S, 1, 1, QUARTER, HALF)
+        mix_d(V, 1, 1, 0, QUARTER)
+        widen4(S, 1, 2)
+        finish(0, 0)
+        quant_d(1, 1)
+        for i in range(4):
+            update(i, 1, 0)
+        for i in range(4):
+            update(i, 1, 1)
+        finish(1, 0)
+        mix_x(S, 1, 2)
+        finish(2, 0)
+        widen4(S, 1, 3)
+        mix_x(S, 1, 3)
+        quant_x(1, 2)
+        finish(3, 0)
+        both(4)
+        finish(0, 1)
+        quant_x(1, 3)
+        finish(1, 1)
+        both(5)
+        finish(2, 1)
+        finish(3, 1)
+        both(6)
+        finish(4, 0)
+        finish(4, 1)
+        both(7)
+        for i in range(5, 8):
+            for half in range(2):
+                finish(i, half)

@@ -33,7 +33,7 @@ def tile_conditionalsyntheticgradientweightupdate_w8_kernel(
         keep = ctx.enter_context(tc.tile_pool(name="keep", bufs=1))
         ring = ctx.enter_context(tc.tile_pool(name="ring", bufs=3))
         psum = ctx.enter_context(tc.psum_pool(name="psum", bufs=1))
-        ctx.enter_context(tc.manual_schedule(engines={mybir.EngineType.SP}))
+        ctx.enter_context(tc.manual_schedule(engines={mybir.EngineType.SP, mybir.EngineType.PE}))
 
         taken = []
 
@@ -93,32 +93,37 @@ def tile_conditionalsyntheticgradientweightupdate_w8_kernel(
             )
 
         def load_c_scales(quad):
-            nc.gpsimd.dma_start(
+            nc.sync.dma_start(
                 out=wt_scales[32 * quad + 8 : 32 * quad + 12, :].bitcast(I32),
                 in_=c_scales[0, 4 * quad : 4 * quad + 4, :].bitcast(I32),
             )
 
         nc.vector.memset(wt_scales[:].bitcast(I32), 0)
         make_identity(nc, ident[:])
-        for quad in range(4):
-            load_c_scales(quad)
 
         load_a(0, 1)
         nc.scalar.dma_start(out=r_raw[:], in_=r.rearrange("(g p j) -> p g j", p=P, j=PACK))
         nc.scalar.dma_start(out=xs_sb[:], in_=x_scale.rearrange("(g p j) o -> p g (j o)", p=P, j=PACK))
         load_x(0, 0)
+        load_m_scales(0)
         load_a(1, 1)
+        load_m_scales(1)
         load_t(0)
         load_a(2, 2)
+        load_m_scales(2)
+        load_m_scales(3)
         load_t(1)
-        for quad in range(4):
-            load_m_scales(quad)
+        load_c_scales(0)
         load_x(0, 1)
-        for q in (2, 0, 1):
-            load_words(q, 0)
+        load_c_scales(1)
+        load_words(0, 0)
+        load_c_scales(2)
+        load_c_scales(3)
+        load_words(1, 0)
+        load_words(2, 0)
         load_a(4, 2)
         load_t(2)
-        for q in (2, 0, 1):
+        for q in range(3):
             load_words(q, 1)
         load_a(6, 2)
         load_t(3)
@@ -129,6 +134,14 @@ def tile_conditionalsyntheticgradientweightupdate_w8_kernel(
 
         nc.scalar.activation(out=r_sb[:], in_=r_raw[:].rearrange("p g j -> p (g j)"), func=COPY)
 
+        idle = keep.tile([P, HALF], BF16, name="idle")
+        nc.vector.memset(idle[:], 0.0)
+        idle_bank = next_bank()
+
+        def warm(count):
+            for i in range(count):
+                nc.tensor.matmul(idle_bank[:], lhsT=idle[:, :P], rhs=idle[:], start=True, stop=True)
+
         k_sb, h_sb, banks, turned, act_codes, act_scales = {}, {}, {}, {}, {}, {}
 
         def slope(s, lo=0, hi=F):
@@ -138,10 +151,16 @@ def tile_conditionalsyntheticgradientweightupdate_w8_kernel(
                 out=k_sb[s][:, lo:hi], in0=a_sb[s][:, lo:hi], scalar1=0.0, scalar2=NEG_SLOPE, op0=ALU.is_gt, op1=ALU.max
             )
 
-        def leaky(s, lo=0, hi=F):
-            if s not in h_sb:
-                h_sb[s] = ring.tile([P, F], BF16, name="h%d" % s, tag="h", align_bytes=64)
-            nc.vector.tensor_tensor(out=h_sb[s][:, lo:hi], in0=a_sb[s][:, lo:hi], in1=k_sb[s][:, lo:hi], op=ALU.mult)
+        def leaky(s, part):
+            if part == 0:
+                h_sb[s] = ring.tile([P, F], BF16, name="h%d" % s, tag="h", bufs=4, align_bytes=64)
+            cols = slice(part * HALF, (part + 1) * HALF)
+            nc.vector.tensor_tensor(
+                out=h_sb[s][:, cols].rearrange("p (u q e) -> p q u e", u=2, e=2),
+                in0=a_sb[s][:, cols].rearrange("p (q u e) -> p q u e", u=2, e=2),
+                in1=k_sb[s][:, cols].rearrange("p (q u e) -> p q u e", u=2, e=2),
+                op=ALU.mult,
+            )
 
         def turn(unit):
             kind, index = unit
@@ -150,9 +169,11 @@ def tile_conditionalsyntheticgradientweightupdate_w8_kernel(
             for part in range(2):
                 for u in range(2):
                     col = (2 * part + u) * P
-                    nc.tensor.transpose(
-                        bank[:, col : col + P], words[:, 2 * P * part + u : 2 * P * (part + 1) : 2], ident[:]
-                    )
+                    if kind == "h":
+                        block = words[:, col : col + P]
+                    else:
+                        block = words[:, 2 * P * part + u : 2 * P * (part + 1) : 2]
+                    nc.tensor.transpose(bank[:, col : col + P], block, ident[:])
             banks[unit] = bank
 
         def drain(unit):
@@ -177,7 +198,7 @@ def tile_conditionalsyntheticgradientweightupdate_w8_kernel(
 
         def predict(s, half):
             bank = next_bank()
-            passes = [(("t", s // 2), s % 2, 2), (("h", s), 0, 0), (("h", s), 1, 1)]
+            passes = [(("h", s), 0, 0), (("h", s), 1, 1), (("t", s // 2), s % 2, 2)]
             for n, (unit, part, q) in enumerate(passes):
                 cols = slice(part * P, (part + 1) * P)
                 nc.tensor.matmul_mx(
@@ -207,8 +228,8 @@ def tile_conditionalsyntheticgradientweightupdate_w8_kernel(
             )
 
         def interleave(engine, mixed, planes, lo, hi):
-            dst = mixed[:].rearrange("p (n j) -> p n j", j=PACK)[:, lo:hi, :]
-            src = planes[:, :, lo:hi].rearrange("p j n -> p n j")
+            dst = mixed[:, lo * PACK : hi * PACK].rearrange("p (c i j) -> p c j i", i=PACK, j=PACK)
+            src = planes[:, :, lo:hi].rearrange("p j (c i) -> p c j i", i=PACK)
             if engine == "vector":
                 nc.vector.tensor_copy(out=dst, in_=src)
             else:
@@ -282,8 +303,9 @@ def tile_conditionalsyntheticgradientweightupdate_w8_kernel(
         def prepare(s):
             slope(s)
             slope(s + 1)
-            leaky(s)
-            leaky(s + 1)
+            for i in range(2):
+                for part in range(2):
+                    leaky(s + i, part)
 
         def units(s):
             return (("h", s), ("t", s // 2), ("h", s + 1))
@@ -297,21 +319,29 @@ def tile_conditionalsyntheticgradientweightupdate_w8_kernel(
                 for half in range(2):
                     update(i, half, g)
 
+        warm(5)
         for s in range(2):
             slope(s, 0, HALF)
             slope(s, HALF, F)
-            leaky(s, 0, HALF)
-            leaky(s, HALF, F)
-            turn(("h", s))
+            leaky(s, 0)
+            leaky(s, 1)
+        turn(("h", 0))
+        warm(2)
         turn(("t", 0))
+        turn(("h", 1))
+        warm(2)
         widen4(S, 0, 1)
         widen4(V, 0, 0)
         drain(("h", 0))
         mix_x(S, 0, 1)
-        drain(("h", 1))
         drain(("t", 0))
+        drain(("h", 1))
         prepare(2)
-        each(turn, units(2))
+        turn(("t", 1))
+        warm(1)
+        turn(("h", 2))
+        warm(1)
+        turn(("h", 3))
         mix_x(V, 0, 0)
         quant_act(("h", 0))
         quant_act(("h", 1))

@@ -33,7 +33,7 @@ def tile_conditionalsyntheticgradientweightupdate_w8_kernel(
         keep = ctx.enter_context(tc.tile_pool(name="keep", bufs=1))
         ring = ctx.enter_context(tc.tile_pool(name="ring", bufs=3))
         psum = ctx.enter_context(tc.psum_pool(name="psum", bufs=1))
-        ctx.enter_context(tc.manual_schedule(engines={mybir.EngineType.SP, mybir.EngineType.PE}))
+        ctx.enter_context(tc.manual_schedule())
 
         taken = []
 
@@ -45,20 +45,20 @@ def tile_conditionalsyntheticgradientweightupdate_w8_kernel(
         a_rows = a.rearrange("(g p j) f -> g p (j f)", p=P, j=PACK)
         t_rows = t.rearrange("(g p j) f -> g p (j f)", p=P, j=PACK)
         x_rows = x_bytes.rearrange("(g p j) f -> g p j f", p=P, j=PACK)
-        a_sb, t_sb, x_sb, w_sb, wt_codes = {}, {}, {}, {}, {}
+        a_sb, blocks, x_sb, w_sb, wt_codes = {}, {}, {}, {}, {}
 
         def load_a(s, count):
             tile = keep.tile([P, count * F], BF16, name="a%d" % s, align_bytes=64)
             g, j = divmod(s, PACK)
             nc.sync.dma_start(out=tile[:], in_=a_rows[g][:, j * F : (j + count) * F])
-            for i in range(count):
-                a_sb[s + i] = tile[:, i * F : (i + 1) * F]
+            a_sb[s] = tile
 
         def load_t(pair):
             tile = keep.tile([P, 2 * T], BF16, name="t%d" % pair, align_bytes=64)
             g, jj = divmod(pair, 2)
             nc.sync.dma_start(out=tile[:], in_=t_rows[g][:, jj * 2 * T : (jj + 1) * 2 * T])
-            t_sb[pair] = tile
+            words = tile[:].bitcast(F32)
+            blocks["t", pair] = [words[:, 2 * P * j + u : 2 * P * (j + 1) : 2] for j in range(2) for u in range(2)]
 
         def load_x(g, side):
             tile = keep.tile([P, PACK, HALF], U8, name="xbytes%d_%d" % (g, side), align_bytes=64)
@@ -98,7 +98,9 @@ def tile_conditionalsyntheticgradientweightupdate_w8_kernel(
                 in_=c_scales[0, 4 * quad : 4 * quad + 4, :].bitcast(I32),
             )
 
-        nc.vector.memset(wt_scales[:].bitcast(I32), 0)
+        nc.gpsimd.memset(wt_scales[:].bitcast(I32), 0)
+        idle = keep.tile([P, HALF], BF16, name="idle")
+        nc.gpsimd.memset(idle[:], 0.0)
         make_identity(nc, ident[:])
 
         load_a(0, 1)
@@ -114,7 +116,7 @@ def tile_conditionalsyntheticgradientweightupdate_w8_kernel(
         load_m_scales(3)
         load_t(1)
         load_c_scales(0)
-        load_x(0, 1)
+        load_x(1, 0)
         load_c_scales(1)
         load_words(0, 0)
         load_c_scales(2)
@@ -123,66 +125,65 @@ def tile_conditionalsyntheticgradientweightupdate_w8_kernel(
         load_words(2, 0)
         load_a(4, 2)
         load_t(2)
+        load_t(3)
+        load_a(6, 2)
         for q in range(3):
             load_words(q, 1)
-        load_a(6, 2)
-        load_t(3)
-        load_x(1, 0)
+        load_x(0, 1)
         load_x(1, 1)
         for pair in range(4):
             load_w(pair)
 
         nc.scalar.activation(out=r_sb[:], in_=r_raw[:].rearrange("p g j -> p (g j)"), func=COPY)
 
-        idle = keep.tile([P, HALF], BF16, name="idle")
-        nc.vector.memset(idle[:], 0.0)
         idle_bank = next_bank()
 
         def warm(count):
             for i in range(count):
                 nc.tensor.matmul(idle_bank[:], lhsT=idle[:, :P], rhs=idle[:], start=True, stop=True)
 
-        k_sb, h_sb, banks, turned, act_codes, act_scales = {}, {}, {}, {}, {}, {}
+        k_sb, k_group, banks, turned, act_q = {}, {}, {}, {}, {}
 
-        def slope(s, lo=0, hi=F):
-            if s not in k_sb:
-                k_sb[s] = keep.tile([P, F], BF16, name="k%d" % s, align_bytes=64)
+        def slope(s):
+            width = a_sb[s].shape[1]
+            tile = keep.tile([P, width], BF16, name="k%d" % s, align_bytes=64)
             nc.vector.tensor_scalar(
-                out=k_sb[s][:, lo:hi], in0=a_sb[s][:, lo:hi], scalar1=0.0, scalar2=NEG_SLOPE, op0=ALU.is_gt, op1=ALU.max
+                out=tile[:], in0=a_sb[s][:], scalar1=0.0, scalar2=NEG_SLOPE, op0=ALU.is_gt, op1=ALU.max
             )
+            k_group[s] = tile
+            for i in range(width // F):
+                k_sb[s + i] = tile[:, i * F : (i + 1) * F]
 
-        def leaky(s, part):
-            if part == 0:
-                h_sb[s] = ring.tile([P, F], BF16, name="h%d" % s, tag="h", bufs=4, align_bytes=64)
-            cols = slice(part * HALF, (part + 1) * HALF)
+        def leaky(s):
+            width = a_sb[s].shape[1]
+            tile = ring.tile([P, width], BF16, name="h%d" % s, tag="h", bufs=3, align_bytes=64)
             nc.vector.tensor_tensor(
-                out=h_sb[s][:, cols].rearrange("p (u q e) -> p q u e", u=2, e=2),
-                in0=a_sb[s][:, cols].rearrange("p (q u e) -> p q u e", u=2, e=2),
-                in1=k_sb[s][:, cols].rearrange("p (q u e) -> p q u e", u=2, e=2),
+                out=tile[:].rearrange("p (u q e) -> p q u e", u=2, e=2),
+                in0=a_sb[s][:].rearrange("p (q u e) -> p q u e", u=2, e=2),
+                in1=k_group[s][:].rearrange("p (q u e) -> p q u e", u=2, e=2),
                 op=ALU.mult,
             )
+            words = tile[:].bitcast(F32).rearrange("p (u b q) -> p u b q", u=2, q=P)
+            for i in range(width // F):
+                blocks["h", s + i] = [words[:, u, 2 * i + part, :] for part in range(2) for u in range(2)]
 
         def turn(unit):
-            kind, index = unit
-            words = (h_sb if kind == "h" else t_sb)[index][:].bitcast(F32)
             bank = next_bank()
-            for part in range(2):
-                for u in range(2):
-                    col = (2 * part + u) * P
-                    if kind == "h":
-                        block = words[:, col : col + P]
-                    else:
-                        block = words[:, 2 * P * part + u : 2 * P * (part + 1) : 2]
-                    nc.tensor.transpose(bank[:, col : col + P], block, ident[:])
+            for n, block in enumerate(blocks[unit]):
+                nc.tensor.transpose(bank[:, n * P : (n + 1) * P], block, ident[:])
             banks[unit] = bank
 
         def drain(unit):
-            tile = ring.tile([P, 2 * HALF], BF16, name="turned_%s%d" % unit, tag="turned", bufs=4, align_bytes=64)
+            kind, index = unit
+            if index % 2 == 0:
+                turned[kind, index // 2] = ring.tile(
+                    [P, 4 * HALF], BF16, name="turned_%s%d" % unit, tag="turned", bufs=3, align_bytes=64
+                )
+            dst = turned[kind, index // 2][:, (index % 2) * 2 * HALF : (index % 2 + 1) * 2 * HALF]
             nc.scalar.copy(
-                out=tile[:].bitcast(F32).rearrange("p (a n u) -> p a n u", a=2, u=2),
+                out=dst.bitcast(F32).rearrange("p (a n u) -> p a n u", a=2, u=2),
                 in_=banks[unit][:].rearrange("p (a u n) -> p a n u", a=2, u=2),
             )
-            turned[unit] = tile
 
         def quantize(name, source):
             width = source.shape[1] // PACK
@@ -191,24 +192,24 @@ def tile_conditionalsyntheticgradientweightupdate_w8_kernel(
             nc.vector.quantize_mx(out=codes[:].bitcast(FP8X4), scales=scales[:], in_=source)
             return codes, scales
 
-        def quant_act(unit):
-            act_codes[unit], act_scales[unit] = quantize("act_%s%d" % unit, turned[unit][:])
+        def quant_act(kind, index):
+            act_q[kind, index] = quantize("act_%s%d" % (kind, index), turned[kind, index][:])
 
         sg_bank, d_planes, d_mixed, d_q = {}, {}, {}, {}
 
         def predict(s, half):
             bank = next_bank()
-            passes = [(("h", s), 0, 0), (("h", s), 1, 1), (("t", s // 2), s % 2, 2)]
-            for n, (unit, part, q) in enumerate(passes):
+            passes = [(("h", s // 2), 2 * (s % 2)), (("h", s // 2), 2 * (s % 2) + 1), (("t", s // PACK), s % PACK)]
+            for q, (unit, part) in enumerate(passes):
                 cols = slice(part * P, (part + 1) * P)
                 nc.tensor.matmul_mx(
                     out=bank[:],
-                    lhsT=act_codes[unit][:, cols].bitcast(FP8X4),
-                    lhsT_scale=act_scales[unit][:, cols],
+                    lhsT=act_q[unit][0][:, cols].bitcast(FP8X4),
+                    lhsT_scale=act_q[unit][1][:, cols],
                     rhs=wt_codes[q, half][:].bitcast(FP8X4),
                     rhs_scale=wt_scales[4 * q :, half * HALF : (half + 1) * HALF],
-                    start=(n == 0),
-                    stop=(n == len(passes) - 1),
+                    start=(q == 0),
+                    stop=(q == len(passes) - 1),
                 )
             sg_bank[s, half] = bank
 
@@ -238,7 +239,7 @@ def tile_conditionalsyntheticgradientweightupdate_w8_kernel(
         def mix_d(engine, g, half, lo, hi):
             if (g, half) not in d_mixed:
                 d_mixed[g, half] = ring.tile(
-                    [P, PACK * HALF], BF16, name="dmix%d_%d" % (g, half), tag="dmix", bufs=2, align_bytes=64
+                    [P, PACK * HALF], BF16, name="dmix%d_%d" % (g, half), tag="dmix", bufs=3, align_bytes=64
                 )
             interleave(engine, d_mixed[g, half], d_planes[g, half], lo, hi)
 
@@ -247,43 +248,41 @@ def tile_conditionalsyntheticgradientweightupdate_w8_kernel(
 
         x_planes, x_mixed, x_q = {}, {}, {}
 
-        def widen(engine, g, piece, j):
-            if j == 0:
-                x_planes[g, piece] = ring.tile(
-                    [P, PACK, QUARTER], BF16, name="xpl%d_%d" % (g, piece), tag="xpl", bufs=4, align_bytes=64
+        def widen(engine, g, side, j):
+            if (g, side) not in x_planes:
+                x_planes[g, side] = ring.tile(
+                    [P, PACK, HALF], BF16, name="xpl%d_%d" % (g, side), tag="xpl", bufs=3, align_bytes=64
                 )
-            side, part = divmod(piece, 2)
-            src = x_sb[g, side][:, j, part * QUARTER : (part + 1) * QUARTER].bitcast(FP8)
-            dst = x_planes[g, piece][:, j, :]
+            dst = x_planes[g, side][:, j, :]
+            src = x_sb[g, side][:, j, :].bitcast(FP8)
+            scale = xs_sb[:, g, j : j + 1]
             if engine == "vector":
-                nc.vector.tensor_scalar(out=dst, in0=src, scalar1=xs_sb[:, g, j : j + 1], scalar2=None, op0=ALU.mult)
+                nc.vector.tensor_scalar(out=dst, in0=src, scalar1=scale, scalar2=None, op0=ALU.mult)
             else:
-                nc.scalar.activation(out=dst, in_=src, func=COPY, scale=xs_sb[:, g, j : j + 1])
+                nc.scalar.activation(out=dst, in_=src, func=COPY, scale=scale)
 
-        def widen4(engine, g, piece):
-            for j in range(PACK):
-                widen(engine, g, piece, j)
+        def mix_x(engine, g, side, lo, hi):
+            if (g, side) not in x_mixed:
+                x_mixed[g, side] = ring.tile(
+                    [P, PACK * HALF], BF16, name="xmix%d_%d" % (g, side), tag="xmix", bufs=3, align_bytes=64
+                )
+            interleave(engine, x_mixed[g, side], x_planes[g, side], lo, hi)
 
-        def mix_x(engine, g, piece):
-            x_mixed[g, piece] = ring.tile(
-                [P, PACK * QUARTER], BF16, name="xmix%d_%d" % (g, piece), tag="xmix", bufs=4, align_bytes=64
-            )
-            interleave(engine, x_mixed[g, piece], x_planes[g, piece], 0, QUARTER)
-
-        def quant_x(g, piece):
-            x_q[g, piece] = quantize("x%d_%d" % (g, piece), x_mixed[g, piece][:])
+        def quant_x(g, side, lo=0, hi=HALF):
+            codes, scales = quantize("x%d_%d_%d" % (g, side, lo), x_mixed[g, side][:, lo * PACK : hi * PACK])
+            for col in range(lo, hi, P):
+                cols = slice(col - lo, col - lo + P)
+                x_q[g, (side * HALF + col) // P] = (codes[:, cols], scales[:, cols])
 
         upd_bank = {}
 
         def update(i, half, g):
             if g == 0:
                 upd_bank[i, half] = next_bank()
-            piece, part = divmod(i, 2)
-            cols = slice(part * P, (part + 1) * P)
             nc.tensor.matmul_mx(
                 out=upd_bank[i, half][:],
-                lhsT=x_q[g, piece][0][:, cols].bitcast(FP8X4),
-                lhsT_scale=x_q[g, piece][1][:, cols],
+                lhsT=x_q[g, i][0].bitcast(FP8X4),
+                lhsT_scale=x_q[g, i][1],
                 rhs=d_q[g, half][0][:].bitcast(FP8X4),
                 rhs_scale=d_q[g, half][1][:],
                 start=(g == 0),
@@ -300,19 +299,13 @@ def tile_conditionalsyntheticgradientweightupdate_w8_kernel(
 
         S, V = "scalar", "vector"
 
-        def prepare(s):
-            slope(s)
-            slope(s + 1)
-            for i in range(2):
-                for part in range(2):
-                    leaky(s + i, part)
+        def turn_two(kind, first):
+            turn((kind, first))
+            turn((kind, first + 1))
 
-        def units(s):
-            return (("h", s), ("t", s // 2), ("h", s + 1))
-
-        def each(step, items):
-            for item in items:
-                step(item)
+        def drain_two(kind, first):
+            drain((kind, first))
+            drain((kind, first + 1))
 
         def both(i):
             for g in range(2):
@@ -320,119 +313,129 @@ def tile_conditionalsyntheticgradientweightupdate_w8_kernel(
                     update(i, half, g)
 
         warm(5)
-        for s in range(2):
-            slope(s, 0, HALF)
-            slope(s, HALF, F)
-            leaky(s, 0)
-            leaky(s, 1)
+        slope(0)
+        leaky(0)
+        widen(V, 0, 0, 0)
+        slope(1)
+        widen(V, 0, 0, 1)
+        leaky(1)
+        widen(S, 0, 0, 2)
+        widen(S, 0, 0, 3)
         turn(("h", 0))
         warm(2)
         turn(("t", 0))
         turn(("h", 1))
         warm(2)
-        widen4(S, 0, 1)
-        widen4(V, 0, 0)
         drain(("h", 0))
-        mix_x(S, 0, 1)
+        mix_x(S, 0, 0, 0, QUARTER)
         drain(("t", 0))
         drain(("h", 1))
-        prepare(2)
+        slope(2)
+        leaky(2)
         turn(("t", 1))
-        warm(1)
-        turn(("h", 2))
-        warm(1)
-        turn(("h", 3))
-        mix_x(V, 0, 0)
-        quant_act(("h", 0))
-        quant_act(("h", 1))
-        quant_act(("t", 0))
+        warm(2)
+        drain(("t", 1))
+        mix_x(S, 0, 0, QUARTER, HALF)
+        quant_act("h", 0)
+        quant_act("t", 0)
+        turn_two("h", 2)
+        drain_two("h", 2)
         predict(0, 0)
         predict(1, 0)
-        widen4(S, 0, 2)
-        each(drain, units(2))
+        widen(V, 1, 0, 0)
+        widen(V, 1, 0, 1)
         quant_x(0, 0)
-        quant_x(0, 1)
-        each(quant_act, units(2))
+        slope(4)
+        quant_act("h", 1)
+        leaky(4)
+        turn_two("t", 2)
+        widen(S, 1, 0, 2)
+        widen(S, 1, 0, 3)
+        drain_two("t", 2)
         predict(2, 0)
         predict(3, 0)
-        mix_x(S, 0, 2)
-        widen4(S, 0, 3)
-        prepare(4)
-        each(turn, units(4))
-        mix_x(S, 0, 3)
-        for s in range(4):
-            grad(s, 0)
-        each(drain, units(4))
+        turn_two("h", 4)
+        mix_x(S, 1, 0, 0, QUARTER)
+        drain_two("h", 4)
+        slope(6)
+        grad(0, 0)
         predict(0, 1)
+        grad(1, 0)
+        leaky(6)
+        turn_two("h", 6)
+        mix_x(S, 1, 0, QUARTER, HALF)
+        drain_two("h", 6)
+        quant_act("t", 1)
+        quant_act("h", 2)
+        grad(2, 0)
         predict(1, 1)
-        prepare(6)
-        each(turn, units(6))
-        mix_d(S, 0, 0, 0, QUARTER)
-        each(quant_act, units(4))
-        each(drain, units(6))
-        grad(0, 1)
-        grad(1, 1)
+        grad(3, 0)
         predict(4, 0)
         predict(5, 0)
-        mix_d(S, 0, 0, QUARTER, HALF)
-        widen4(S, 1, 0)
-        each(quant_act, units(6))
+        quant_act("h", 3)
         predict(6, 0)
         predict(7, 0)
-        quant_x(0, 2)
-        quant_x(0, 3)
-        mix_x(S, 1, 0)
-        quant_d(0, 0)
+        mix_d(S, 0, 0, 0, HALF)
+        grad(0, 1)
+        grad(1, 1)
+        quant_x(1, 0)
         for s in range(4, 8):
             grad(s, 0)
-        predict(2, 1)
-        predict(3, 1)
-        for s in range(4, 8):
-            predict(s, 1)
-        widen4(S, 1, 1)
+        for j in range(PACK):
+            widen(S, 0, 1, j)
         mix_d(S, 1, 0, 0, HALF)
-        quant_x(1, 0)
+        for s in range(2, 6):
+            predict(s, 1)
+        quant_d(0, 0)
         grad(2, 1)
         grad(3, 1)
+        for s in range(6, 8):
+            predict(s, 1)
         mix_d(S, 0, 1, 0, HALF)
-        mix_x(V, 1, 1)
         grad(4, 1)
-        quant_d(1, 0)
         grad(5, 1)
-        quant_x(1, 1)
+        quant_d(1, 0)
         for i in range(4):
             update(i, 0, 0)
             update(i, 0, 1)
-        grad(6, 1)
-        grad(7, 1)
-        quant_d(0, 1)
-        mix_d(S, 1, 1, QUARTER, HALF)
-        mix_d(V, 1, 1, 0, QUARTER)
-        widen4(S, 1, 2)
+        for s in range(6, 8):
+            grad(s, 1)
+        for j in range(2):
+            widen(S, 1, 1, j)
+        mix_d(S, 1, 1, 0, QUARTER)
         finish(0, 0)
-        quant_d(1, 1)
+        mix_d(V, 1, 1, QUARTER, HALF)
+        quant_d(0, 1)
         for i in range(4):
             update(i, 1, 0)
+        for j in range(2, PACK):
+            widen(S, 1, 1, j)
+        finish(1, 0)
+        quant_d(1, 1)
         for i in range(4):
             update(i, 1, 1)
-        finish(1, 0)
-        mix_x(S, 1, 2)
+        mix_x(S, 0, 1, 0, QUARTER)
+        mix_x(S, 1, 1, 0, QUARTER)
+        mix_x(S, 0, 1, QUARTER, HALF)
+        mix_x(S, 1, 1, QUARTER, HALF)
         finish(2, 0)
-        widen4(S, 1, 3)
-        mix_x(S, 1, 3)
-        quant_x(1, 2)
         finish(3, 0)
-        both(4)
         finish(0, 1)
-        quant_x(1, 3)
+        quant_x(0, 1, 0, QUARTER)
         finish(1, 1)
-        both(5)
+        quant_x(1, 1, 0, QUARTER)
+        both(4)
         finish(2, 1)
         finish(3, 1)
-        both(6)
+        both(5)
+        quant_x(0, 1, QUARTER, HALF)
         finish(4, 0)
+        quant_x(1, 1, QUARTER, HALF)
+        both(6)
         finish(4, 1)
+        finish(5, 0)
         both(7)
-        for i in range(5, 8):
+        finish(5, 1)
+        for i in range(6, 8):
             for half in range(2):
                 finish(i, half)

@@ -19,10 +19,13 @@ COPY = mybir.ActivationFunctionType.Copy
 P = 128
 PACK = 4
 HALF = 512
-QUARTER = 256
+QUARTER = HALF // 2
 BANKS = 8
+QUADRANT = 32
+SCALE_ROWS = 4
 NEG_SLOPE = 0.25
 STEP = -1.0 / 32.0
+VECTOR_PLANES = 2
 
 
 def tile_conditionalsyntheticgradientweightupdate_w8_kernel(
@@ -35,12 +38,15 @@ def tile_conditionalsyntheticgradientweightupdate_w8_kernel(
         psum = ctx.enter_context(tc.psum_pool(name="psum", bufs=1))
         ctx.enter_context(tc.manual_schedule())
 
-        taken = []
+        free_banks = list(range(BANKS))
+        bank_of = {}
 
-        def next_bank():
-            bank = psum.tile([P, HALF], F32, name="bank%d" % len(taken), tag="bank%d" % (len(taken) % BANKS))
-            taken.append(bank)
-            return bank
+        def take_bank(user):
+            bank_of[user] = free_banks.pop(0)
+            return psum.tile([P, HALF], F32, name="bank_%s%d_%d" % user, tag="bank%d" % bank_of[user])
+
+        def give_bank(user):
+            free_banks.append(bank_of[user])
 
         a_rows = a.rearrange("(g p j) f -> g p (j f)", p=P, j=PACK)
         t_rows = t.rearrange("(g p j) f -> g p (j f)", p=P, j=PACK)
@@ -55,10 +61,10 @@ def tile_conditionalsyntheticgradientweightupdate_w8_kernel(
 
         def load_t(pair):
             tile = keep.tile([P, 2 * T], BF16, name="t%d" % pair, align_bytes=64)
-            g, jj = divmod(pair, 2)
-            nc.sync.dma_start(out=tile[:], in_=t_rows[g][:, jj * 2 * T : (jj + 1) * 2 * T])
+            g, within = divmod(pair, 2)
+            nc.sync.dma_start(out=tile[:], in_=t_rows[g][:, within * 2 * T : (within + 1) * 2 * T])
             words = tile[:].bitcast(F32)
-            blocks["t", pair] = [words[:, 2 * P * j + u : 2 * P * (j + 1) : 2] for j in range(2) for u in range(2)]
+            blocks["t", pair] = [words[:, 2 * P * n + u : 2 * P * (n + 1) : 2] for n in range(2) for u in range(2)]
 
         def load_x(g, side):
             tile = keep.tile([P, PACK, HALF], U8, name="xbytes%d_%d" % (g, side), align_bytes=64)
@@ -87,20 +93,22 @@ def tile_conditionalsyntheticgradientweightupdate_w8_kernel(
         xs_sb = keep.tile([P, 2, PACK], F32, name="xs_sb")
 
         def load_m_scales(quad):
+            first = QUADRANT * quad
             nc.sync.dma_start(
-                out=wt_scales[32 * quad : 32 * quad + 8, :].bitcast(I32),
-                in_=m_scales[:, 4 * quad : 4 * quad + 4, :].bitcast(I32),
+                out=wt_scales[first : first + 2 * SCALE_ROWS, :].bitcast(I32),
+                in_=m_scales[:, SCALE_ROWS * quad : SCALE_ROWS * (quad + 1), :].bitcast(I32),
             )
 
         def load_c_scales(quad):
+            first = QUADRANT * quad + 2 * SCALE_ROWS
             nc.sync.dma_start(
-                out=wt_scales[32 * quad + 8 : 32 * quad + 12, :].bitcast(I32),
-                in_=c_scales[0, 4 * quad : 4 * quad + 4, :].bitcast(I32),
+                out=wt_scales[first : first + SCALE_ROWS, :].bitcast(I32),
+                in_=c_scales[0, SCALE_ROWS * quad : SCALE_ROWS * (quad + 1), :].bitcast(I32),
             )
 
         nc.gpsimd.memset(wt_scales[:].bitcast(I32), 0)
-        idle = keep.tile([P, HALF], BF16, name="idle")
-        nc.gpsimd.memset(idle[:], 0.0)
+        zeros = keep.tile([P, HALF], BF16, name="zeros")
+        nc.gpsimd.memset(zeros[:], 0.0)
         make_identity(nc, ident[:])
 
         load_a(0, 1)
@@ -127,22 +135,23 @@ def tile_conditionalsyntheticgradientweightupdate_w8_kernel(
         load_t(2)
         load_t(3)
         load_a(6, 2)
-        for q in range(3):
+        for q in range(len(word_sources)):
             load_words(q, 1)
         load_x(0, 1)
         load_x(1, 1)
-        for pair in range(4):
+        for pair in range(D // (2 * P)):
             load_w(pair)
 
         nc.scalar.activation(out=r_sb[:], in_=r_raw[:].rearrange("p g j -> p (g j)"), func=COPY)
 
-        idle_bank = next_bank()
+        warm_user = ("warm", 0, 0)
+        warm_bank = take_bank(warm_user)
 
         def warm(count):
-            for i in range(count):
-                nc.tensor.matmul(idle_bank[:], lhsT=idle[:, :P], rhs=idle[:], start=True, stop=True)
+            for unused in range(count):
+                nc.tensor.matmul(warm_bank[:], lhsT=zeros[:, :P], rhs=zeros[:], start=True, stop=True)
 
-        k_sb, k_group, banks, turned, act_q = {}, {}, {}, {}, {}
+        k_sb, k_loaded, turn_bank, turned, act_q = {}, {}, {}, {}, {}
 
         def slope(s):
             width = a_sb[s].shape[1]
@@ -150,40 +159,49 @@ def tile_conditionalsyntheticgradientweightupdate_w8_kernel(
             nc.vector.tensor_scalar(
                 out=tile[:], in0=a_sb[s][:], scalar1=0.0, scalar2=NEG_SLOPE, op0=ALU.is_gt, op1=ALU.max
             )
-            k_group[s] = tile
+            k_loaded[s] = tile
             for i in range(width // F):
                 k_sb[s + i] = tile[:, i * F : (i + 1) * F]
 
         def leaky(s):
             width = a_sb[s].shape[1]
-            tile = ring.tile([P, width], BF16, name="h%d" % s, tag="h", bufs=3, align_bytes=64)
+            tile = ring.tile([P, width], BF16, name="h%d" % s, tag="h", align_bytes=64)
             nc.vector.tensor_tensor(
                 out=tile[:].rearrange("p (u q e) -> p q u e", u=2, e=2),
                 in0=a_sb[s][:].rearrange("p (q u e) -> p q u e", u=2, e=2),
-                in1=k_group[s][:].rearrange("p (q u e) -> p q u e", u=2, e=2),
+                in1=k_loaded[s][:].rearrange("p (q u e) -> p q u e", u=2, e=2),
                 op=ALU.mult,
             )
             words = tile[:].bitcast(F32).rearrange("p (u b q) -> p u b q", u=2, q=P)
             for i in range(width // F):
-                blocks["h", s + i] = [words[:, u, 2 * i + part, :] for part in range(2) for u in range(2)]
+                blocks["h", s + i] = [words[:, u, 2 * i + n, :] for n in range(2) for u in range(2)]
 
-        def turn(unit):
-            bank = next_bank()
-            for n, block in enumerate(blocks[unit]):
+        def turn(kind, index):
+            bank = take_bank((kind, index, 0))
+            for n, block in enumerate(blocks[kind, index]):
                 nc.tensor.transpose(bank[:, n * P : (n + 1) * P], block, ident[:])
-            banks[unit] = bank
+            turn_bank[kind, index] = bank
 
-        def drain(unit):
-            kind, index = unit
-            if index % 2 == 0:
-                turned[kind, index // 2] = ring.tile(
-                    [P, 4 * HALF], BF16, name="turned_%s%d" % unit, tag="turned", bufs=3, align_bytes=64
+        def drain(kind, index):
+            duo, place = divmod(index, 2)
+            if place == 0:
+                turned[kind, duo] = ring.tile(
+                    [P, 4 * HALF], BF16, name="turned_%s%d" % (kind, index), tag="turned", align_bytes=64
                 )
-            dst = turned[kind, index // 2][:, (index % 2) * 2 * HALF : (index % 2 + 1) * 2 * HALF]
+            dst = turned[kind, duo][:, place * 2 * HALF : (place + 1) * 2 * HALF]
             nc.scalar.copy(
-                out=dst.bitcast(F32).rearrange("p (a n u) -> p a n u", a=2, u=2),
-                in_=banks[unit][:].rearrange("p (a u n) -> p a n u", a=2, u=2),
+                out=dst.bitcast(F32).rearrange("p (n c u) -> p n c u", n=2, u=2),
+                in_=turn_bank[kind, index][:].rearrange("p (n u c) -> p n c u", n=2, u=2),
             )
+            give_bank((kind, index, 0))
+
+        def turn_two(kind, first):
+            turn(kind, first)
+            turn(kind, first + 1)
+
+        def drain_two(kind, first):
+            drain(kind, first)
+            drain(kind, first + 1)
 
         def quantize(name, source):
             width = source.shape[1] // PACK
@@ -192,24 +210,28 @@ def tile_conditionalsyntheticgradientweightupdate_w8_kernel(
             nc.vector.quantize_mx(out=codes[:].bitcast(FP8X4), scales=scales[:], in_=source)
             return codes, scales
 
-        def quant_act(kind, index):
-            act_q[kind, index] = quantize("act_%s%d" % (kind, index), turned[kind, index][:])
+        def quant_act(kind, duo):
+            act_q[kind, duo] = quantize("act_%s%d" % (kind, duo), turned[kind, duo][:])
 
         sg_bank, d_planes, d_mixed, d_q = {}, {}, {}, {}
 
         def predict(s, half):
-            bank = next_bank()
-            passes = [(("h", s // 2), 2 * (s % 2)), (("h", s // 2), 2 * (s % 2) + 1), (("t", s // PACK), s % PACK)]
-            for q, (unit, part) in enumerate(passes):
-                cols = slice(part * P, (part + 1) * P)
+            bank = take_bank(("sg", s, half))
+            stationary = [
+                (act_q["h", s // 2], 2 * (s % 2)),
+                (act_q["h", s // 2], 2 * (s % 2) + 1),
+                (act_q["t", s // PACK], s % PACK),
+            ]
+            for q, ((codes, scales), slot) in enumerate(stationary):
+                cols = slice(slot * P, (slot + 1) * P)
                 nc.tensor.matmul_mx(
                     out=bank[:],
-                    lhsT=act_q[unit][0][:, cols].bitcast(FP8X4),
-                    lhsT_scale=act_q[unit][1][:, cols],
+                    lhsT=codes[:, cols].bitcast(FP8X4),
+                    lhsT_scale=scales[:, cols],
                     rhs=wt_codes[q, half][:].bitcast(FP8X4),
-                    rhs_scale=wt_scales[4 * q :, half * HALF : (half + 1) * HALF],
+                    rhs_scale=wt_scales[SCALE_ROWS * q :, half * HALF : (half + 1) * HALF],
                     start=(q == 0),
-                    stop=(q == len(passes) - 1),
+                    stop=(q == len(stationary) - 1),
                 )
             sg_bank[s, half] = bank
 
@@ -217,7 +239,7 @@ def tile_conditionalsyntheticgradientweightupdate_w8_kernel(
             g, j = divmod(s, PACK)
             if j == 0:
                 d_planes[g, half] = ring.tile(
-                    [P, PACK, HALF], BF16, name="dpl%d_%d" % (g, half), tag="dpl", bufs=3, align_bytes=64
+                    [P, PACK, HALF], BF16, name="dpl%d_%d" % (g, half), tag="dpl", bufs=4, align_bytes=64
                 )
             nc.vector.scalar_tensor_tensor(
                 out=d_planes[g, half][:, j, :],
@@ -227,46 +249,61 @@ def tile_conditionalsyntheticgradientweightupdate_w8_kernel(
                 op0=ALU.mult,
                 op1=ALU.mult,
             )
+            give_bank(("sg", s, half))
 
-        def interleave(engine, mixed, planes, lo, hi):
-            dst = mixed[:, lo * PACK : hi * PACK].rearrange("p (c i j) -> p c j i", i=PACK, j=PACK)
-            src = planes[:, :, lo:hi].rearrange("p j (c i) -> p c j i", i=PACK)
-            if engine == "vector":
-                nc.vector.tensor_copy(out=dst, in_=src)
-            else:
-                nc.scalar.copy(out=dst, in_=src)
+        def interleave(mixed, planes, lo, hi):
+            nc.scalar.copy(
+                out=mixed[:, lo * PACK : hi * PACK].rearrange("p (c i j) -> p c j i", i=PACK, j=PACK),
+                in_=planes[:, :, lo:hi].rearrange("p j (c i) -> p c j i", i=PACK),
+            )
 
-        def mix_d(engine, g, half, lo, hi):
-            if (g, half) not in d_mixed:
-                d_mixed[g, half] = ring.tile(
-                    [P, PACK * HALF], BF16, name="dmix%d_%d" % (g, half), tag="dmix", bufs=3, align_bytes=64
-                )
-            interleave(engine, d_mixed[g, half], d_planes[g, half], lo, hi)
+        def mix_d(g, half):
+            d_mixed[g, half] = ring.tile(
+                [P, PACK * HALF], BF16, name="dmix%d_%d" % (g, half), tag="dmix", align_bytes=64
+            )
+            interleave(d_mixed[g, half], d_planes[g, half], 0, HALF)
 
         def quant_d(g, half):
             d_q[g, half] = quantize("d%d_%d" % (g, half), d_mixed[g, half][:])
 
-        x_planes, x_mixed, x_q = {}, {}, {}
+        x_planes, x_mixed, x_q, upd_bank = {}, {}, {}, {}
 
-        def widen(engine, g, side, j):
-            if (g, side) not in x_planes:
+        def widen_operands(g, side, j):
+            if j == 0:
                 x_planes[g, side] = ring.tile(
-                    [P, PACK, HALF], BF16, name="xpl%d_%d" % (g, side), tag="xpl", bufs=3, align_bytes=64
+                    [P, PACK, HALF], BF16, name="xpl%d_%d" % (g, side), tag="xpl", align_bytes=64
                 )
-            dst = x_planes[g, side][:, j, :]
-            src = x_sb[g, side][:, j, :].bitcast(FP8)
-            scale = xs_sb[:, g, j : j + 1]
-            if engine == "vector":
-                nc.vector.tensor_scalar(out=dst, in0=src, scalar1=scale, scalar2=None, op0=ALU.mult)
-            else:
+            return x_planes[g, side][:, j, :], x_sb[g, side][:, j, :].bitcast(FP8), xs_sb[:, g, j : j + 1]
+
+        def widen_on_vector(g, side, j):
+            dst, src, scale = widen_operands(g, side, j)
+            nc.vector.tensor_scalar(out=dst, in0=src, scalar1=scale, scalar2=None, op0=ALU.mult)
+
+        def widen_on_scalar(g, side, planes):
+            for j in planes:
+                dst, src, scale = widen_operands(g, side, j)
                 nc.scalar.activation(out=dst, in_=src, func=COPY, scale=scale)
 
-        def mix_x(engine, g, side, lo, hi):
-            if (g, side) not in x_mixed:
-                x_mixed[g, side] = ring.tile(
-                    [P, PACK * HALF], BF16, name="xmix%d_%d" % (g, side), tag="xmix", bufs=3, align_bytes=64
-                )
-            interleave(engine, x_mixed[g, side], x_planes[g, side], lo, hi)
+        def new_x_mixed(g, side):
+            x_mixed[g, side] = ring.tile(
+                [P, PACK * HALF], BF16, name="xmix%d_%d" % (g, side), tag="xmix", align_bytes=64
+            )
+
+        def mix_x(g, side, lo):
+            if lo == 0:
+                new_x_mixed(g, side)
+            interleave(x_mixed[g, side], x_planes[g, side], lo, lo + QUARTER)
+
+        def mix_x_on_gpsimd(g, side):
+            new_x_mixed(g, side)
+            nc.gpsimd.tensor_scalar(
+                out=x_mixed[g, side][:].rearrange("p (n j) -> p n j", j=PACK),
+                in0=x_planes[g, side][:].rearrange("p j n -> p n j"),
+                scalar1=1.0,
+                scalar2=0.0,
+                op0=ALU.mult,
+                op1=ALU.add,
+            )
 
         def quant_x(g, side, lo=0, hi=HALF):
             codes, scales = quantize("x%d_%d_%d" % (g, side, lo), x_mixed[g, side][:, lo * PACK : hi * PACK])
@@ -274,11 +311,9 @@ def tile_conditionalsyntheticgradientweightupdate_w8_kernel(
                 cols = slice(col - lo, col - lo + P)
                 x_q[g, (side * HALF + col) // P] = (codes[:, cols], scales[:, cols])
 
-        upd_bank = {}
-
         def update(i, half, g):
             if g == 0:
-                upd_bank[i, half] = next_bank()
+                upd_bank[i, half] = take_bank(("upd", i, half))
             nc.tensor.matmul_mx(
                 out=upd_bank[i, half][:],
                 lhsT=x_q[g, i][0].bitcast(FP8X4),
@@ -289,73 +324,65 @@ def tile_conditionalsyntheticgradientweightupdate_w8_kernel(
                 stop=(g == 1),
             )
 
+        def update_both_halves(i, g):
+            update(i, 0, g)
+            update(i, 1, g)
+
         def finish(i, half):
             cols = slice(half * HALF, (half + 1) * HALF)
-            result = ring.tile([P, HALF], F32, name="res%d_%d" % (i, half), tag="res", bufs=8)
+            result = keep.tile([P, HALF], F32, name="res%d_%d" % (i, half))
             nc.vector.scalar_tensor_tensor(
                 out=result[:], in0=upd_bank[i, half][:], scalar=STEP, in1=w_sb[i][:, cols], op0=ALU.mult, op1=ALU.add
             )
+            give_bank(("upd", i, half))
             nc.sync.dma_start(out=out[i * P : (i + 1) * P, cols], in_=result[:])
 
-        S, V = "scalar", "vector"
-
-        def turn_two(kind, first):
-            turn((kind, first))
-            turn((kind, first + 1))
-
-        def drain_two(kind, first):
-            drain((kind, first))
-            drain((kind, first + 1))
-
-        def both(i):
-            for g in range(2):
-                for half in range(2):
-                    update(i, half, g)
+        scalar_planes = range(VECTOR_PLANES, PACK)
 
         warm(5)
         slope(0)
         leaky(0)
-        widen(V, 0, 0, 0)
+        widen_on_vector(0, 0, 0)
         slope(1)
-        widen(V, 0, 0, 1)
+        widen_on_vector(0, 0, 1)
         leaky(1)
-        widen(S, 0, 0, 2)
-        widen(S, 0, 0, 3)
-        turn(("h", 0))
+        widen_on_scalar(0, 0, scalar_planes)
+        turn("h", 0)
         warm(2)
-        turn(("t", 0))
-        turn(("h", 1))
+        turn("t", 0)
+        turn("h", 1)
         warm(2)
-        drain(("h", 0))
-        mix_x(S, 0, 0, 0, QUARTER)
-        drain(("t", 0))
-        drain(("h", 1))
+        drain("h", 0)
+        mix_x(0, 0, 0)
+        drain("t", 0)
+        drain("h", 1)
         slope(2)
         leaky(2)
-        turn(("t", 1))
+        turn("t", 1)
         warm(2)
-        drain(("t", 1))
-        mix_x(S, 0, 0, QUARTER, HALF)
+        give_bank(warm_user)
+        drain("t", 1)
+        mix_x(0, 0, QUARTER)
         quant_act("h", 0)
         quant_act("t", 0)
         turn_two("h", 2)
         drain_two("h", 2)
+
         predict(0, 0)
         predict(1, 0)
-        widen(V, 1, 0, 0)
-        widen(V, 1, 0, 1)
+        for j in range(VECTOR_PLANES):
+            widen_on_vector(1, 0, j)
         quant_x(0, 0)
         slope(4)
         quant_act("h", 1)
         leaky(4)
         turn_two("t", 2)
-        widen(S, 1, 0, 2)
-        widen(S, 1, 0, 3)
+        widen_on_scalar(1, 0, scalar_planes)
         drain_two("t", 2)
         predict(2, 0)
         predict(3, 0)
         turn_two("h", 4)
-        mix_x(S, 1, 0, 0, QUARTER)
+        mix_x(1, 0, 0)
         drain_two("h", 4)
         slope(6)
         grad(0, 0)
@@ -363,79 +390,77 @@ def tile_conditionalsyntheticgradientweightupdate_w8_kernel(
         grad(1, 0)
         leaky(6)
         turn_two("h", 6)
-        mix_x(S, 1, 0, QUARTER, HALF)
+        mix_x(1, 0, QUARTER)
         drain_two("h", 6)
         quant_act("t", 1)
         quant_act("h", 2)
         grad(2, 0)
         predict(1, 1)
         grad(3, 0)
+
         predict(4, 0)
         predict(5, 0)
         quant_act("h", 3)
+        quant_x(1, 0)
         predict(6, 0)
         predict(7, 0)
-        mix_d(S, 0, 0, 0, HALF)
+        widen_on_scalar(0, 1, range(PACK))
+        mix_x_on_gpsimd(0, 1)
+        mix_d(0, 0)
+        widen_on_scalar(1, 1, range(1))
         grad(0, 1)
         grad(1, 1)
-        quant_x(1, 0)
         for s in range(4, 8):
             grad(s, 0)
-        for j in range(PACK):
-            widen(S, 0, 1, j)
-        mix_d(S, 1, 0, 0, HALF)
+        mix_d(1, 0)
         for s in range(2, 6):
             predict(s, 1)
-        quant_d(0, 0)
         grad(2, 1)
         grad(3, 1)
         for s in range(6, 8):
             predict(s, 1)
-        mix_d(S, 0, 1, 0, HALF)
+        mix_d(0, 1)
         grad(4, 1)
+        quant_d(0, 0)
         grad(5, 1)
         quant_d(1, 0)
+
         for i in range(4):
             update(i, 0, 0)
             update(i, 0, 1)
-        for s in range(6, 8):
-            grad(s, 1)
-        for j in range(2):
-            widen(S, 1, 1, j)
-        mix_d(S, 1, 1, 0, QUARTER)
+        grad(6, 1)
+        grad(7, 1)
+        mix_d(1, 1)
+        quant_x(0, 1)
+        update(4, 0, 0)
+        update(5, 0, 0)
         finish(0, 0)
-        mix_d(V, 1, 1, QUARTER, HALF)
+        finish(1, 0)
         quant_d(0, 1)
         for i in range(4):
             update(i, 1, 0)
-        for j in range(2, PACK):
-            widen(S, 1, 1, j)
-        finish(1, 0)
+        widen_on_scalar(1, 1, range(1, PACK))
+        finish(2, 0)
         quant_d(1, 1)
         for i in range(4):
             update(i, 1, 1)
-        mix_x(S, 0, 1, 0, QUARTER)
-        mix_x(S, 1, 1, 0, QUARTER)
-        mix_x(S, 0, 1, QUARTER, HALF)
-        mix_x(S, 1, 1, QUARTER, HALF)
-        finish(2, 0)
         finish(3, 0)
+        update(4, 1, 0)
+        update(5, 1, 0)
+        mix_x(1, 1, 0)
+        mix_x(1, 1, QUARTER)
         finish(0, 1)
-        quant_x(0, 1, 0, QUARTER)
         finish(1, 1)
-        quant_x(1, 1, 0, QUARTER)
-        both(4)
+        update_both_halves(6, 0)
         finish(2, 1)
+        quant_x(1, 1, 0, QUARTER)
+        update_both_halves(4, 1)
+        update_both_halves(5, 1)
         finish(3, 1)
-        both(5)
-        quant_x(0, 1, QUARTER, HALF)
-        finish(4, 0)
+        update_both_halves(7, 0)
         quant_x(1, 1, QUARTER, HALF)
-        both(6)
-        finish(4, 1)
-        finish(5, 0)
-        both(7)
-        finish(5, 1)
-        for i in range(6, 8):
-            for half in range(2):
-                finish(i, half)
+        update_both_halves(6, 1)
+        update_both_halves(7, 1)
+        for i in range(4, 8):
+            finish(i, 0)
+            finish(i, 1)

from contextlib import ExitStack

import concourse.mybir as mybir
from concourse.masks import make_identity

N, D, F, T = 1024, 1024, 1024, 512
FLOPS = 2 * N * F * (F + T) + 2 * N * D * F

F32 = mybir.dt.float32
BF16 = mybir.dt.bfloat16
I32 = mybir.dt.int32
U32 = mybir.dt.uint32
U8 = mybir.dt.uint8
FP8 = mybir.dt.float8_e4m3fn
FP8X4 = mybir.dt.float8_e4m3fn_x4
ALU = mybir.AluOpType
COPY = mybir.ActivationFunctionType.Copy

P = 128
PACK = 4
HALF = 512
QUARTER = HALF // 2
BANKS = 8
QUADRANT = 32
SCALE_ROWS = 4
NEG_SLOPE = 0.25
STEP = -1.0 / 32.0
VECTOR_PLANES = 2


def tile_conditionalsyntheticgradientweightupdate_w8_kernel(
    tc, x_bytes, x_scale, a, m_words, m_scales, t, c_words, c_scales, r, w, out
):
    nc = tc.nc
    with ExitStack() as ctx:
        keep = ctx.enter_context(tc.tile_pool(name="keep", bufs=1))
        ring = ctx.enter_context(tc.tile_pool(name="ring", bufs=3))
        psum = ctx.enter_context(tc.psum_pool(name="psum", bufs=1))
        ctx.enter_context(tc.manual_schedule())

        free_banks = list(range(BANKS))
        bank_of = {}

        def take_bank(user):
            bank_of[user] = free_banks.pop(0)
            return psum.tile([P, HALF], F32, name="bank_%s%d_%d" % user, tag="bank%d" % bank_of[user])

        def give_bank(user):
            free_banks.append(bank_of[user])

        a_rows = a.rearrange("(g p j) f -> g p (j f)", p=P, j=PACK)
        t_rows = t.rearrange("(g p j) f -> g p (j f)", p=P, j=PACK)
        x_rows = x_bytes.rearrange("(g p j) f -> g p j f", p=P, j=PACK)
        a_sb, blocks, x_sb, w_sb, wt_codes = {}, {}, {}, {}, {}

        def load_a(s, count):
            tile = keep.tile([P, count * F], BF16, name="a%d" % s, align_bytes=64)
            g, j = divmod(s, PACK)
            nc.sync.dma_start(out=tile[:], in_=a_rows[g][:, j * F : (j + count) * F])
            a_sb[s] = tile

        def load_t(pair):
            tile = keep.tile([P, 2 * T], BF16, name="t%d" % pair, align_bytes=64)
            g, within = divmod(pair, 2)
            nc.sync.dma_start(out=tile[:], in_=t_rows[g][:, within * 2 * T : (within + 1) * 2 * T])
            words = tile[:].bitcast(F32)
            blocks["t", pair] = [words[:, 2 * P * n + u : 2 * P * (n + 1) : 2] for n in range(2) for u in range(2)]

        def load_x(g, side):
            tile = keep.tile([P, PACK, HALF], U8, name="xbytes%d_%d" % (g, side), align_bytes=64)
            nc.sync.dma_start(out=tile[:], in_=x_rows[g][:, :, side * HALF : (side + 1) * HALF])
            x_sb[g, side] = tile

        def load_w(pair):
            tile = keep.tile([P, 2, F], BF16, name="w%d" % pair, align_bytes=64)
            rows = w[pair * 2 * P : (pair + 1) * 2 * P, :].rearrange("(i p) f -> p i f", p=P)
            nc.sync.dma_start(out=tile[:], in_=rows)
            w_sb[2 * pair] = tile[:, 0, :]
            w_sb[2 * pair + 1] = tile[:, 1, :]

        word_sources = [m_words[0], m_words[1], c_words[0]]

        def load_words(q, half):
            tile = keep.tile([P, HALF], U32, name="words%d_%d" % (q, half), align_bytes=64)
            src = word_sources[q].rearrange("p n t -> p (n t)")[:, half * HALF * PACK : (half + 1) * HALF * PACK]
            nc.sync.dma_start(out=tile[:].bitcast(I32), in_=src.bitcast(I32))
            wt_codes[q, half] = tile

        wt_scales = keep.tile([P, F], U8, name="wt_scales", align_bytes=64)
        ident = keep.tile([P, P], F32, name="ident")
        r_raw = keep.tile([P, 2, PACK], BF16, name="r_raw")
        r_sb = keep.tile([P, 2 * PACK], F32, name="r_sb")
        xs_sb = keep.tile([P, 2, PACK], F32, name="xs_sb")

        def load_m_scales(quad):
            first = QUADRANT * quad
            nc.sync.dma_start(
                out=wt_scales[first : first + 2 * SCALE_ROWS, :].bitcast(I32),
                in_=m_scales[:, SCALE_ROWS * quad : SCALE_ROWS * (quad + 1), :].bitcast(I32),
            )

        def load_c_scales(quad):
            first = QUADRANT * quad + 2 * SCALE_ROWS
            nc.sync.dma_start(
                out=wt_scales[first : first + SCALE_ROWS, :].bitcast(I32),
                in_=c_scales[0, SCALE_ROWS * quad : SCALE_ROWS * (quad + 1), :].bitcast(I32),
            )

        nc.gpsimd.memset(wt_scales[:].bitcast(I32), 0)
        zeros = keep.tile([P, HALF], BF16, name="zeros")
        nc.gpsimd.memset(zeros[:], 0.0)
        make_identity(nc, ident[:])

        load_a(0, 1)
        nc.scalar.dma_start(out=r_raw[:], in_=r.rearrange("(g p j) -> p g j", p=P, j=PACK))
        nc.scalar.dma_start(out=xs_sb[:], in_=x_scale.rearrange("(g p j) o -> p g (j o)", p=P, j=PACK))
        load_x(0, 0)
        load_m_scales(0)
        load_a(1, 1)
        load_m_scales(1)
        load_t(0)
        load_a(2, 2)
        load_m_scales(2)
        load_m_scales(3)
        load_t(1)
        load_c_scales(0)
        load_x(1, 0)
        load_c_scales(1)
        load_words(0, 0)
        load_c_scales(2)
        load_c_scales(3)
        load_words(1, 0)
        load_words(2, 0)
        load_a(4, 2)
        load_t(2)
        load_t(3)
        load_a(6, 2)
        for q in range(len(word_sources)):
            load_words(q, 1)
        load_x(0, 1)
        load_x(1, 1)
        for pair in range(D // (2 * P)):
            load_w(pair)

        nc.scalar.activation(out=r_sb[:], in_=r_raw[:].rearrange("p g j -> p (g j)"), func=COPY)

        warm_user = ("warm", 0, 0)
        warm_bank = take_bank(warm_user)

        def warm(count):
            for unused in range(count):
                nc.tensor.matmul(warm_bank[:], lhsT=zeros[:, :P], rhs=zeros[:], start=True, stop=True)

        k_sb, k_loaded, turn_bank, turned, act_q = {}, {}, {}, {}, {}

        def slope(s):
            width = a_sb[s].shape[1]
            tile = keep.tile([P, width], BF16, name="k%d" % s, align_bytes=64)
            nc.vector.tensor_scalar(
                out=tile[:], in0=a_sb[s][:], scalar1=0.0, scalar2=NEG_SLOPE, op0=ALU.is_gt, op1=ALU.max
            )
            k_loaded[s] = tile
            for i in range(width // F):
                k_sb[s + i] = tile[:, i * F : (i + 1) * F]

        def leaky(s):
            width = a_sb[s].shape[1]
            tile = ring.tile([P, width], BF16, name="h%d" % s, tag="h", align_bytes=64)
            nc.vector.tensor_tensor(
                out=tile[:].rearrange("p (u q e) -> p q u e", u=2, e=2),
                in0=a_sb[s][:].rearrange("p (q u e) -> p q u e", u=2, e=2),
                in1=k_loaded[s][:].rearrange("p (q u e) -> p q u e", u=2, e=2),
                op=ALU.mult,
            )
            words = tile[:].bitcast(F32).rearrange("p (u b q) -> p u b q", u=2, q=P)
            for i in range(width // F):
                blocks["h", s + i] = [words[:, u, 2 * i + n, :] for n in range(2) for u in range(2)]

        def turn(kind, index):
            bank = take_bank((kind, index, 0))
            for n, block in enumerate(blocks[kind, index]):
                nc.tensor.transpose(bank[:, n * P : (n + 1) * P], block, ident[:])
            turn_bank[kind, index] = bank

        def drain(kind, index):
            duo, place = divmod(index, 2)
            if place == 0:
                turned[kind, duo] = ring.tile(
                    [P, 4 * HALF], BF16, name="turned_%s%d" % (kind, index), tag="turned", align_bytes=64
                )
            dst = turned[kind, duo][:, place * 2 * HALF : (place + 1) * 2 * HALF]
            nc.scalar.copy(
                out=dst.bitcast(F32).rearrange("p (n c u) -> p n c u", n=2, u=2),
                in_=turn_bank[kind, index][:].rearrange("p (n u c) -> p n c u", n=2, u=2),
            )
            give_bank((kind, index, 0))

        def turn_two(kind, first):
            turn(kind, first)
            turn(kind, first + 1)

        def drain_two(kind, first):
            drain(kind, first)
            drain(kind, first + 1)

        def quantize(name, source):
            width = source.shape[1] // PACK
            codes = keep.tile([P, width], U32, name=name + "_codes", align_bytes=64)
            scales = keep.tile([P, width], U8, name=name + "_scales", align_bytes=64)
            nc.vector.quantize_mx(out=codes[:].bitcast(FP8X4), scales=scales[:], in_=source)
            return codes, scales

        def quant_act(kind, duo):
            act_q[kind, duo] = quantize("act_%s%d" % (kind, duo), turned[kind, duo][:])

        sg_bank, d_planes, d_mixed, d_q = {}, {}, {}, {}

        def predict(s, half):
            bank = take_bank(("sg", s, half))
            stationary = [
                (act_q["h", s // 2], 2 * (s % 2)),
                (act_q["h", s // 2], 2 * (s % 2) + 1),
                (act_q["t", s // PACK], s % PACK),
            ]
            for q, ((codes, scales), slot) in enumerate(stationary):
                cols = slice(slot * P, (slot + 1) * P)
                nc.tensor.matmul_mx(
                    out=bank[:],
                    lhsT=codes[:, cols].bitcast(FP8X4),
                    lhsT_scale=scales[:, cols],
                    rhs=wt_codes[q, half][:].bitcast(FP8X4),
                    rhs_scale=wt_scales[SCALE_ROWS * q :, half * HALF : (half + 1) * HALF],
                    start=(q == 0),
                    stop=(q == len(stationary) - 1),
                )
            sg_bank[s, half] = bank

        def grad(s, half):
            g, j = divmod(s, PACK)
            if j == 0:
                d_planes[g, half] = ring.tile(
                    [P, PACK, HALF], BF16, name="dpl%d_%d" % (g, half), tag="dpl", bufs=4, align_bytes=64
                )
            nc.vector.scalar_tensor_tensor(
                out=d_planes[g, half][:, j, :],
                in0=sg_bank[s, half][:],
                scalar=r_sb[:, s : s + 1],
                in1=k_sb[s][:, half * HALF : (half + 1) * HALF],
                op0=ALU.mult,
                op1=ALU.mult,
            )
            give_bank(("sg", s, half))

        def interleave(mixed, planes, lo, hi):
            nc.scalar.copy(
                out=mixed[:, lo * PACK : hi * PACK].rearrange("p (c i j) -> p c j i", i=PACK, j=PACK),
                in_=planes[:, :, lo:hi].rearrange("p j (c i) -> p c j i", i=PACK),
            )

        def mix_d(g, half):
            d_mixed[g, half] = ring.tile(
                [P, PACK * HALF], BF16, name="dmix%d_%d" % (g, half), tag="dmix", align_bytes=64
            )
            interleave(d_mixed[g, half], d_planes[g, half], 0, HALF)

        def quant_d(g, half):
            d_q[g, half] = quantize("d%d_%d" % (g, half), d_mixed[g, half][:])

        x_planes, x_mixed, x_q, upd_bank = {}, {}, {}, {}

        def widen_operands(g, side, j):
            if j == 0:
                x_planes[g, side] = ring.tile(
                    [P, PACK, HALF], BF16, name="xpl%d_%d" % (g, side), tag="xpl", align_bytes=64
                )
            return x_planes[g, side][:, j, :], x_sb[g, side][:, j, :].bitcast(FP8), xs_sb[:, g, j : j + 1]

        def widen_on_vector(g, side, j):
            dst, src, scale = widen_operands(g, side, j)
            nc.vector.tensor_scalar(out=dst, in0=src, scalar1=scale, scalar2=None, op0=ALU.mult)

        def widen_on_scalar(g, side, planes):
            for j in planes:
                dst, src, scale = widen_operands(g, side, j)
                nc.scalar.activation(out=dst, in_=src, func=COPY, scale=scale)

        def new_x_mixed(g, side):
            x_mixed[g, side] = ring.tile(
                [P, PACK * HALF], BF16, name="xmix%d_%d" % (g, side), tag="xmix", align_bytes=64
            )

        def mix_x(g, side, lo):
            if lo == 0:
                new_x_mixed(g, side)
            interleave(x_mixed[g, side], x_planes[g, side], lo, lo + QUARTER)

        def mix_x_on_gpsimd(g, side):
            new_x_mixed(g, side)
            nc.gpsimd.tensor_scalar(
                out=x_mixed[g, side][:].rearrange("p (n j) -> p n j", j=PACK),
                in0=x_planes[g, side][:].rearrange("p j n -> p n j"),
                scalar1=1.0,
                scalar2=0.0,
                op0=ALU.mult,
                op1=ALU.add,
            )

        def quant_x(g, side, lo=0, hi=HALF):
            codes, scales = quantize("x%d_%d_%d" % (g, side, lo), x_mixed[g, side][:, lo * PACK : hi * PACK])
            for col in range(lo, hi, P):
                cols = slice(col - lo, col - lo + P)
                x_q[g, (side * HALF + col) // P] = (codes[:, cols], scales[:, cols])

        def update(i, half, g):
            if g == 0:
                upd_bank[i, half] = take_bank(("upd", i, half))
            nc.tensor.matmul_mx(
                out=upd_bank[i, half][:],
                lhsT=x_q[g, i][0].bitcast(FP8X4),
                lhsT_scale=x_q[g, i][1],
                rhs=d_q[g, half][0][:].bitcast(FP8X4),
                rhs_scale=d_q[g, half][1][:],
                start=(g == 0),
                stop=(g == 1),
            )

        def update_both_halves(i, g):
            update(i, 0, g)
            update(i, 1, g)

        def finish(i, half):
            cols = slice(half * HALF, (half + 1) * HALF)
            result = keep.tile([P, HALF], F32, name="res%d_%d" % (i, half))
            nc.vector.scalar_tensor_tensor(
                out=result[:], in0=upd_bank[i, half][:], scalar=STEP, in1=w_sb[i][:, cols], op0=ALU.mult, op1=ALU.add
            )
            give_bank(("upd", i, half))
            nc.sync.dma_start(out=out[i * P : (i + 1) * P, cols], in_=result[:])

        scalar_planes = range(VECTOR_PLANES, PACK)

        warm(5)
        slope(0)
        leaky(0)
        widen_on_vector(0, 0, 0)
        slope(1)
        widen_on_vector(0, 0, 1)
        leaky(1)
        widen_on_scalar(0, 0, scalar_planes)
        turn("h", 0)
        warm(2)
        turn("t", 0)
        turn("h", 1)
        warm(2)
        drain("h", 0)
        mix_x(0, 0, 0)
        drain("t", 0)
        drain("h", 1)
        slope(2)
        leaky(2)
        turn("t", 1)
        warm(2)
        give_bank(warm_user)
        drain("t", 1)
        mix_x(0, 0, QUARTER)
        quant_act("h", 0)
        quant_act("t", 0)
        turn_two("h", 2)
        drain_two("h", 2)

        predict(0, 0)
        predict(1, 0)
        for j in range(VECTOR_PLANES):
            widen_on_vector(1, 0, j)
        quant_x(0, 0)
        slope(4)
        quant_act("h", 1)
        leaky(4)
        turn_two("t", 2)
        widen_on_scalar(1, 0, scalar_planes)
        drain_two("t", 2)
        predict(2, 0)
        predict(3, 0)
        turn_two("h", 4)
        mix_x(1, 0, 0)
        drain_two("h", 4)
        slope(6)
        grad(0, 0)
        predict(0, 1)
        grad(1, 0)
        leaky(6)
        turn_two("h", 6)
        mix_x(1, 0, QUARTER)
        drain_two("h", 6)
        quant_act("t", 1)
        quant_act("h", 2)
        grad(2, 0)
        predict(1, 1)
        grad(3, 0)

        predict(4, 0)
        predict(5, 0)
        quant_act("h", 3)
        quant_x(1, 0)
        predict(6, 0)
        predict(7, 0)
        widen_on_scalar(0, 1, range(PACK))
        mix_x_on_gpsimd(0, 1)
        mix_d(0, 0)
        widen_on_scalar(1, 1, range(1))
        grad(0, 1)
        grad(1, 1)
        for s in range(4, 8):
            grad(s, 0)
        mix_d(1, 0)
        for s in range(2, 6):
            predict(s, 1)
        grad(2, 1)
        grad(3, 1)
        for s in range(6, 8):
            predict(s, 1)
        mix_d(0, 1)
        grad(4, 1)
        quant_d(0, 0)
        grad(5, 1)
        quant_d(1, 0)

        for i in range(4):
            update(i, 0, 0)
            update(i, 0, 1)
        grad(6, 1)
        grad(7, 1)
        mix_d(1, 1)
        quant_x(0, 1)
        update(4, 0, 0)
        update(5, 0, 0)
        finish(0, 0)
        finish(1, 0)
        quant_d(0, 1)
        for i in range(4):
            update(i, 1, 0)
        widen_on_scalar(1, 1, range(1, PACK))
        finish(2, 0)
        quant_d(1, 1)
        for i in range(4):
            update(i, 1, 1)
        finish(3, 0)
        update(4, 1, 0)
        update(5, 1, 0)
        mix_x(1, 1, 0)
        mix_x(1, 1, QUARTER)
        finish(0, 1)
        finish(1, 1)
        update_both_halves(6, 0)
        finish(2, 1)
        quant_x(1, 1, 0, QUARTER)
        update_both_halves(4, 1)
        update_both_halves(5, 1)
        finish(3, 1)
        update_both_halves(7, 0)
        quant_x(1, 1, QUARTER, HALF)
        update_both_halves(6, 1)
        update_both_halves(7, 1)
        for i in range(4, 8):
            finish(i, 0)
            finish(i, 1)
